import numpy as np
import ml_dtypes


def mxq(x, axis, fmt="e4m3"):
    dtype, down = {"e4m3": (ml_dtypes.float8_e4m3fn, 7), "e5m2": (ml_dtypes.float8_e5m2, 14)}[fmt]
    v = np.moveaxis(np.asarray(x, np.float32).astype(ml_dtypes.bfloat16).astype(np.float64), axis, -1)
    blocks = v.reshape(v.shape[:-1] + (-1, 32))
    amax = np.abs(blocks).max(-1, keepdims=True)
    byte = np.maximum(np.where(amax > 0, np.frexp(amax)[1] - 1 + 127, 0) - down, 1)
    scale = np.exp2(byte - 127.0)
    codes = (blocks / scale).astype(np.float32).astype(dtype).astype(np.float64)
    return np.moveaxis((codes * scale).reshape(v.shape), -1, axis)


WIDE = False


def mx_kscale(k):
    if not WIDE:
        return np.ones(k)
    levels = np.array([10, -10, 5, -5, 0])
    if k % 512:
        return np.exp2(np.random.permutation(np.resize(levels, k // 32))).repeat(32)
    a = np.empty((k // 512, 16))
    for p in range(k // 512):
        a[p, :8] = np.random.permutation(np.resize(levels, 8))
        for g in range(8):
            far = levels[np.abs(levels - a[p, g]) >= 10]
            a[p, g + 8] = far[np.random.randint(len(far))]
    return np.exp2(a.ravel()).repeat(32)


def f64(x):
    return np.asarray(x).astype(np.float64)


def striped(idx):
    return np.tile(np.asarray(idx).reshape(-1, 16).T, (8, 1)).astype(np.uint16)


def unstriped(offs):
    return offs[:16].T.reshape(-1).astype(np.int64)


def striped8(idx):
    return np.asarray(idx).reshape(8, -1, 16).transpose(0, 2, 1).reshape(128, -1).astype(np.uint16)


def unstriped8(offs):
    return offs.reshape(8, 16, -1).transpose(0, 2, 1).reshape(8, -1).astype(np.int64)


def pick8(x, idx, run):
    r = np.arange(len(x))
    return x[r[:, None], idx[r % (8 * run) // run]]


E2M1 = np.array([0.0, 0.5, 1.0, 1.5, 2.0, 3.0, 4.0, 6.0, -0.0, -0.5, -1.0, -1.5, -2.0, -3.0, -4.0, -6.0])


def pack_weight(w, fmt):
    k, n = w.shape
    w = f64(np.asarray(w, np.float32).astype(ml_dtypes.bfloat16)).reshape(k // 32, 32, n)
    amax = np.abs(w).max(1)
    if fmt == "e4m3":
        byte = np.frexp(amax)[1] - 1 + 127 - 7
    else:
        mant, ex = np.frexp(amax / 6.0)
        byte = np.where(mant > 0.5, ex, ex - 1) + 127
    byte = np.clip(np.where(amax > 0, byte, 1), 1, 254)
    scaled = (w * np.exp2(127.0 - byte)[:, None, :]).reshape(k, n).astype(np.float32)
    by_word = np.ascontiguousarray(scaled.reshape(k // 512, 128, 4, n).transpose(0, 1, 3, 2))
    if fmt == "e4m3":
        words = by_word.astype(ml_dtypes.float8_e4m3fn).view(np.uint8)
    else:
        c = by_word.astype(ml_dtypes.float4_e2m1fn).view(np.uint8) & 0xF
        words = (c[..., 0::2] | (c[..., 1::2] << 4)).reshape(k // 512, 128, 2 * n)
    return np.ascontiguousarray(words), np.ascontiguousarray(byte.astype(np.uint8).reshape(k // 512, 16, n))


def unpack_weight(words, scales, fmt):
    g, _, n = scales.shape
    words = np.ascontiguousarray(words).reshape(g, 128, n, -1)
    if fmt == "e4m3":
        vals = words.view(ml_dtypes.float8_e4m3fn).astype(np.float64)
    else:
        nib = np.empty((g, 128, n, 4), np.uint8)
        nib[..., 0::2] = words & 0xF
        nib[..., 1::2] = words >> 4
        vals = E2M1[nib]
    vals = vals * np.repeat(np.exp2(scales.astype(np.float64) - 127.0), 8, axis=1)[..., None]
    return vals.transpose(0, 1, 3, 2).reshape(g * 512, n)


K, J, R, T, C, D, N, S = 512, 256, 512, 1024, 512, 1024, 256, 1024


def setup_inputs():
    n = np.random.standard_normal
    idx = np.random.permutation(T)[:J]
    idx2 = np.stack([np.random.permutation(C)[:J] for _ in range(8)])
    idx3 = np.stack([np.random.permutation(C)[:J] for _ in range(8)])
    idx4 = np.random.permutation(S)[:N]
    fk = mx_kscale(K)
    fr = mx_kscale(R)
    xtp = pack_weight(n((K, T)) * fk[:, None], "e2m1")
    wp = pack_weight(n((K, R)) * 1 / np.sqrt(K) / fk[:, None] * fr, "e4m3")
    w2p = pack_weight(n((K, R)) * 1 / np.sqrt(K) / fk[:, None] * fr, "e4m3")
    vsp = pack_weight(n((R, S)) * 1 / np.sqrt(R) / fr[:, None], "e2m1")
    return {
        "xt_words": xtp[0],
        "xt_scales": xtp[1],
        "w_words": wp[0],
        "w_scales": wp[1],
        "w2_words": w2p[0],
        "w2_scales": w2p[1],
        "vs_words": vsp[0],
        "vs_scales": vsp[1],
        "offs": striped(idx),
        "offs2": striped8(idx2),
        "offs3": striped8(idx3),
        "offs4": striped(idx4),
    }


def reference(xt_words, xt_scales, w_words, w_scales, w2_words, w2_scales, vs_words, vs_scales, offs, offs2, offs3, offs4):
    idx = unstriped(offs)
    idx2 = unstriped8(offs2)
    idx3 = unstriped8(offs3)
    idx4 = unstriped(offs4)
    xtu = unpack_weight(xt_words, xt_scales, "e2m1")
    wu = unpack_weight(w_words, w_scales, "e4m3")
    w2u = unpack_weight(w2_words, w2_scales, "e4m3")
    vsu = unpack_weight(vs_words, vs_scales, "e2m1")
    xtidxg = xtu[:, idx]
    a = wu.T @ xtidxg
    b = w2u.T @ xtidxg
    pw = np.zeros((R, C))
    pw[np.arange(R)[:, None], idx2[np.arange(R) % 512 // 64]] = a
    pv = np.zeros((R, C))
    pv[np.arange(R)[:, None], idx3[np.arange(R) % 512 // 64]] = b
    g1 = np.maximum(pw, pv)
    g2 = np.abs(pw - pv)
    hid = np.concatenate([g1, g2], axis=1)
    vsidx4g = vsu[:, idx4]
    hidq = mxq(hid, 0, "e4m3")
    y = vsidx4g.T @ hidq
    return y

from contextlib import ExitStack

import concourse.mybir as mybir

K, J, R, T, C, D, N, S = 512, 256, 512, 1024, 512, 1024, 256, 1024
FLOPS = 2 * K * R * J * 2 + 2 * R * N * D

F32 = mybir.dt.float32
BF16 = mybir.dt.bfloat16
I32 = mybir.dt.int32
U32 = mybir.dt.uint32
U16 = mybir.dt.uint16
U8 = mybir.dt.uint8
FP8X4 = mybir.dt.float8_e4m3fn_x4
FP4X4 = mybir.dt.float4_e2m1fn_x4
ALU = mybir.AluOpType
ACT = mybir.ActivationFunctionType

P = 128
PACK = 4
QUADS = 4
HALF = J // 2
CH = C // 2


def tile_picked_tokens_plain_twin_sidepages_store_plain_kernel(
    tc, xt_words, xt_scales, w_words, w_scales, w2_words, w2_scales, vs_words, vs_scales, offs, offs2, offs3, offs4, out
):
    nc = tc.nc
    with ExitStack() as ctx:
        lists = ctx.enter_context(tc.tile_pool(name="lists", bufs=1))
        sb = ctx.enter_context(tc.tile_pool(name="sb", bufs=1))
        psum = ctx.enter_context(tc.psum_pool(name="psum", bufs=1))

        def tile(name, shape, dtype):
            return sb.tile(shape, dtype, name=name, align_bytes=64)

        def bank(name, index, shape):
            return psum.tile(shape, F32, name=name, tag="bank%d" % index)

        def load_scale_rows(plane, scales, quadrants):
            for q in quadrants:
                nc.sync.dma_start(
                    out=plane[32 * q : 32 * q + 4, :].bitcast(I32), in_=scales[0, 4 * q : 4 * q + 4, :].bitcast(I32)
                )

        idx = lists.tile([P, J // 16], U16, name="idx")
        idx2 = lists.tile([P, J // 16], U16, name="idx2")
        idx3 = lists.tile([P, J // 16], U16, name="idx3")
        idx4 = lists.tile([P, N // 16], U16, name="idx4")

        xt_w = sb.tile([P, T], U16, name="xt_w", tag="fp4_words", align_bytes=64)
        xt_s = tile("xt_s", [P, T], U8)
        vs_s = tile("vs_s", [P, S], U8)
        w_w = [tile("w_w0", [P, R], U32)]
        w_s = [tile("w_s%d" % m, [P, R], U8) for m in range(2)]
        w_stage = sb.tile([4, 2, R], U8, name="w_stage", tag="early_rows", align_bytes=64)
        pages = [[tile("page%d_%d" % (m, t), [P, C], F32) for t in range(PACK)] for m in range(2)]

        nc.vector.memset(xt_s[:].bitcast(I32), 0)
        nc.vector.memset(w_s[0][:].bitcast(I32), 0)
        nc.vector.memset(w_s[1][:].bitcast(I32), 0)
        nc.vector.memset(vs_s[:].bitcast(I32), 0)
        for t in range(PACK):
            for m in range(2):
                nc.vector.memset(pages[m][t][:], 0.0)

        nc.sync.dma_start(idx[:], offs)
        nc.sync.dma_start(
            out=w_stage[:].bitcast(I32), in_=w_scales[0, 0:8].rearrange("(q i) c -> i q c", i=4).bitcast(I32)
        )
        nc.sync.dma_start(idx2[:], offs2)
        nc.sync.dma_start(idx3[:], offs3)
        nc.sync.dma_start(idx4[:], offs4)
        nc.sync.dma_start(out=xt_w[:].bitcast(I32), in_=xt_words[0].bitcast(I32))
        nc.sync.dma_start(out=w_w[0][:].bitcast(I32), in_=w_words[0].rearrange("p c j -> p (c j)").bitcast(I32))
        load_scale_rows(xt_s, xt_scales, range(QUADS))
        load_scale_rows(w_s[0], w_scales, (2, 3))
        load_scale_rows(w_s[1], w2_scales, range(QUADS))

        xg_w = tile("xg_w", [P, J], U16)
        xg_s = tile("xg_s", [P, J], U8)
        vg_w = tile("vg_w", [P, N], U16)
        vg_s = tile("vg_s", [P, N], U8)
        wd_w = [tile("wd_w%d" % m, [P, R], U32) for m in range(2)]
        wd_s = [tile("wd_s%d" % m, [P, R], U8) for m in range(2)]

        def gather(dst, window, offsets, lo, hi):
            nc.vector.tensor_copy(dst[:, lo:hi], window[:].indirect(offsets[:, lo // 16 : hi // 16]))

        def deal(dst, src, m, t0, t1):
            nc.vector.tensor_copy(
                dst[m][:, t0 * P : t1 * P].rearrange("p (t m) -> p m t", m=P),
                src[m][:].rearrange("p (m t) -> p m t", t=PACK)[:, :, t0:t1],
            )

        def product(dst, m, t, lo, hi):
            nc.tensor.matmul_mx(
                out=dst,
                lhsT=wd_w[m][:, t * P : (t + 1) * P].bitcast(FP8X4),
                lhsT_scale=wd_s[m][:, t * P : (t + 1) * P],
                rhs=xg_w[:, lo:hi].bitcast(FP4X4),
                rhs_scale=xg_s[:, lo:hi],
                start=True,
                stop=True,
            )

        page_list = (idx2, idx3)

        def scatter(values, m, t, lo, hi):
            nc.scalar.activation(pages[m][t][:].indirect(page_list[m][:, lo // 16 : hi // 16]), values, ACT.Copy)

        def products_out(items, lo, hi, index):
            acc = bank("acc%d" % index, index, [P, len(items), hi - lo])
            held = tile("res%d" % index, [P, len(items), hi - lo], F32)
            for n, (m, t) in enumerate(items):
                product(acc[:, n, :], m, t, lo, hi)
            nc.vector.tensor_copy(held[:], acc[:])
            for n, (m, t) in enumerate(items):
                scatter(held[:, n, :], m, t, lo, hi)

        for q in range(2):
            nc.vector.tensor_copy(w_s[0][32 * q : 32 * q + 4, :].bitcast(I32), w_stage[:, q, :].bitcast(I32))
        w_w.append(sb.tile([P, R], U32, name="w_w1", tag="early_rows", align_bytes=64))
        nc.sync.dma_start(out=w_w[1][:].bitcast(I32), in_=w2_words[0].rearrange("p c j -> p (c j)").bitcast(I32))
        load_scale_rows(vs_s, vs_scales, range(QUADS))
        gather(xg_w, xt_w, idx, 0, HALF)
        deal(wd_w, w_w, 0, 0, 1)
        gather(xg_s, xt_s, idx, 0, HALF)
        deal(wd_s, w_s, 0, 0, 1)
        first = bank("first", 0, [P, HALF])
        first_res = tile("first_res", [P, HALF], F32)
        product(first[:], 0, 0, 0, HALF)
        nc.scalar.activation(first_res[:], first[:], ACT.Copy)
        scatter(first_res[:], 0, 0, 0, HALF)

        gather(xg_s, xt_s, idx, HALF, J)
        gather(xg_w, xt_w, idx, HALF, J)
        vs_w = sb.tile([P, S], U16, name="vs_w", tag="fp4_words", align_bytes=64)
        nc.sync.dma_start(out=vs_w[:].bitcast(I32), in_=vs_words[0].bitcast(I32))
        deal(wd_s, w_s, 0, 1, 2)
        products_out([(0, 0)], HALF, J, 1)
        deal(wd_w, w_w, 0, 1, 2)
        products_out([(0, 1)], 0, J, 2)
        deal(wd_s, w_s, 1, 0, 4)
        deal(wd_w, w_w, 1, 0, 4)
        products_out([(1, 0), (1, 1)], 0, J, 3)
        deal(wd_s, w_s, 0, 2, 4)
        deal(wd_w, w_w, 0, 2, 4)
        products_out([(0, 2), (1, 2)], 0, J, 4)
        products_out([(0, 3), (1, 3)], 0, J, 5)
        gather(vg_s, vs_s, idx4, 0, N)
        gather(vg_w, vs_w, idx4, 0, N)

        larger_planes = tile("larger_planes", [P, PACK, C], BF16)
        diffs = [tile("diffs%d" % u, [P, 2, C], F32) for u in range(2)]
        hid = [tile("hid%d" % k, [P, CH, PACK], BF16) for k in range(4)]
        codes = [tile("codes%d" % k, [P, CH], U32) for k in range(4)]
        scales = [tile("scales%d" % k, [P, CH], U8) for k in range(4)]
        halves = [slice(h * CH, (h + 1) * CH) for h in range(2)]
        whole = slice(0, C)

        def larger(t, cols):
            nc.vector.tensor_tensor(larger_planes[:, t, cols], pages[0][t][:, cols], pages[1][t][:, cols], ALU.max)

        def difference(t, cols):
            nc.vector.tensor_tensor(diffs[t // 2][:, t % 2, cols], pages[0][t][:, cols], pages[1][t][:, cols], ALU.subtract)

        def diff_view(u, h):
            return diffs[u][:, :, halves[h]].rearrange("p e c -> p c e")

        def weave(h, t0, t1):
            nc.vector.tensor_copy(hid[h][:, :, t0:t1], larger_planes[:, t0:t1, halves[h]].rearrange("p t c -> p c t"))

        def quantize(k):
            nc.vector.quantize_mx(
                out=codes[k][:].bitcast(FP8X4), scales=scales[k][:], in_=hid[k][:].rearrange("p c t -> p (c t)")
            )

        for t in range(PACK - 1):
            difference(t, whole)
            larger(t, whole)
            if t == 1:
                for h in range(2):
                    nc.vector.scalar_tensor_tensor(
                        hid[2 + h][:, :, 0:2], diff_view(0, h), -1.0, diff_view(0, h), ALU.mult, ALU.max
                    )
        for h in range(2):
            weave(h, 0, 3)
        for h in range(2):
            difference(3, halves[h])
            nc.scalar.activation(hid[2 + h][:, :, 2:4], diff_view(1, h), ACT.Abs)
        for h in range(2):
            larger(3, halves[h])
        quantize(2)
        weave(0, 3, 4)
        weave(1, 3, 4)
        quantize(0)
        quantize(3)
        quantize(1)

        out_v = out.rearrange("(u p) d -> p u d", p=P)

        def final_product(dst, k, u):
            nc.tensor.matmul_mx(
                out=dst,
                lhsT=vg_w[:, u * P : (u + 1) * P].bitcast(FP4X4),
                lhsT_scale=vg_s[:, u * P : (u + 1) * P],
                rhs=codes[k][:].bitcast(FP8X4),
                rhs_scale=scales[k][:],
                start=True,
                stop=True,
            )

        for n, k in enumerate((2, 0, 3, 1)):
            y = tile("y%d" % k, [P, 2, CH], F32)
            if n < 3:
                acc = bank("yacc%d" % k, 1 + n, [P, 2, CH])
                for u in range(2):
                    final_product(acc[:, u, :], k, u)
                if n < 2:
                    nc.scalar.copy(y[:], acc[:])
                else:
                    nc.vector.tensor_copy(y[:], acc[:])
            else:
                for u in range(2):
                    acc = bank("yacc%d_%d" % (k, u), 4 + u, [P, CH])
                    final_product(acc[:], k, u)
                    if u == 0:
                        nc.scalar.copy(y[:, u, :], acc[:])
                    else:
                        nc.vector.tensor_copy(y[:, u, :], acc[:])
            nc.sync.dma_start(out=out_v[:, :, k * CH : (k + 1) * CH], in_=y[:])
